import numpy as np
import ml_dtypes


def mxq(x, axis, fmt="e4m3"):
    dtype, down = {"e4m3": (ml_dtypes.float8_e4m3fn, 7), "e5m2": (ml_dtypes.float8_e5m2, 14)}[fmt]
    v = np.moveaxis(np.asarray(x, np.float32).astype(ml_dtypes.bfloat16).astype(np.float64), axis, -1)
    blocks = v.reshape(v.shape[:-1] + (-1, 32))
    amax = np.abs(blocks).max(-1, keepdims=True)
    byte = np.maximum(np.where(amax > 0, np.frexp(amax)[1] - 1 + 127, 0) - down, 1)
    scale = np.exp2(byte - 127.0)
    codes = (blocks / scale).astype(np.float32).astype(dtype).astype(np.float64)
    return np.moveaxis((codes * scale).reshape(v.shape), -1, axis)


WIDE = False


def mx_kscale(k):
    if not WIDE:
        return np.ones(k)
    levels = np.array([10, -10, 5, -5, 0])
    if k % 512:
        return np.exp2(np.random.permutation(np.resize(levels, k // 32))).repeat(32)
    a = np.empty((k // 512, 16))
    for p in range(k // 512):
        a[p, :8] = np.random.permutation(np.resize(levels, 8))
        for g in range(8):
            far = levels[np.abs(levels - a[p, g]) >= 10]
            a[p, g + 8] = far[np.random.randint(len(far))]
    return np.exp2(a.ravel()).repeat(32)


def f64(x):
    return np.asarray(x).astype(np.float64)


def striped(idx):
    return np.tile(idx.reshape(-1, 16).T, (8, 1)).astype(np.uint16)


def unstriped(offs):
    return offs[:16].T.reshape(-1).astype(np.int64)


def pack_weight(w):
    k, n = w.shape
    w = f64(np.asarray(w, np.float32).astype(ml_dtypes.bfloat16)).reshape(k // 32, 32, n)
    amax = np.abs(w).max(1)
    byte = np.clip(np.where(amax > 0, np.frexp(amax)[1] - 1 + 127 - 7, 1), 1, 254)
    scaled = (w * np.exp2(127.0 - byte)[:, None, :]).reshape(k, n).astype(np.float32)
    words = np.ascontiguousarray(scaled.reshape(k // 512, 128, 4, n).transpose(0, 1, 3, 2)).astype(ml_dtypes.float8_e4m3fn).view(np.uint8)
    return words, np.ascontiguousarray(byte.astype(np.uint8).reshape(k // 512, 16, n))


def unpack_weight(words, scales):
    g, p, n, _ = words.shape
    vals = np.ascontiguousarray(words).view(ml_dtypes.float8_e4m3fn).astype(np.float64) * np.repeat(np.exp2(scales.astype(np.float64) - 127.0), 8, axis=1)[..., None]
    return vals.transpose(0, 1, 3, 2).reshape(g * 512, n)


K, T, S, N, H = 512, 1024, 512, 256, 512


def setup_inputs():
    n = np.random.standard_normal
    s = mx_kscale(K)[:, None]
    u = mx_kscale(H)
    packed_xT = pack_weight(n((K, T)) * s)
    return {
        "x_words": packed_xT[0],
        "x_scales": packed_xT[1],
        "w1": (n((K, H)) / np.sqrt(K) / s).astype(np.float32),
        "rdy": (np.random.uniform(0.0, 1.0, (H, S))).astype(np.float32),
        "unit": (np.random.uniform(0.6, 1.4, (H, 1)) * u[:, None]).astype(np.float32),
        "w2": (n((H, N)) / np.sqrt(H) / u[:, None]).astype(np.float32),
        "offs": striped(np.random.permutation(T)[:S]),
        "pr1": striped(np.random.permutation(S)),
        "pr2": striped(np.random.permutation(S)),
    }


def reference(x_words, x_scales, w1, rdy, unit, w2, offs, pr1, pr2):
    xq = unpack_weight(x_words, x_scales)[:, unstriped(offs)]
    y = mxq(f64(w1), 0, "e4m3").T @ xq
    dur = np.log(np.exp(y) + 1.0)
    fin0 = dur + f64(rdy)
    fa = fin0[:, unstriped(pr1)]
    fb = fin0[:, unstriped(pr2)]
    fin1 = dur + np.maximum(fa, fb)
    fc = fin1[:, unstriped(pr1)]
    fd = fin1[:, unstriped(pr2)]
    fin2 = dur + np.maximum(fc, fd)
    hid = f64(unit) * fin2
    return mxq(f64(w2), 0, "e4m3").T @ mxq(hid, 0, "e4m3")

@@ -1,0 +1,236 @@
+from contextlib import ExitStack
+import math
+
+import concourse.mybir as mybir
+from concourse.masks import make_identity
+
+K, T, S, N, H = 512, 1024, 512, 256, 512
+FLOPS = 2 * K * H * S + 2 * H * N * S
+
+F32 = mybir.dt.float32
+BF16 = mybir.dt.bfloat16
+I32 = mybir.dt.int32
+U32 = mybir.dt.uint32
+U16 = mybir.dt.uint16
+U8 = mybir.dt.uint8
+FP8X4 = mybir.dt.float8_e4m3fn_x4
+ALU = mybir.AluOpType
+ACT = mybir.ActivationFunctionType
+
+P = 128
+PACK = 4
+KNEE = 32.0
+HALF = H // 2
+CHUNKS = (128, 256, 128,)
+R1_ON_VECTOR = {(0, 1), (1, 1), (2, 1)}
+R2_ON_VECTOR = {(1, 1)}
+WHOLE = 3
+
+
+def tile_picked_ycritp_fin_p_kernel(
+    tc, x_words, x_scales, w1, rdy, unit, w2, offs, pr1, pr2, out
+):
+    nc = tc.nc
+    with ExitStack() as ctx:
+        keep = ctx.enter_context(tc.tile_pool(name="keep", bufs=1))
+        psum = ctx.enter_context(tc.psum_pool(name="psum", bufs=1))
+
+        def gather(on_vector, dst, window, offsets):
+            if on_vector:
+                nc.vector.tensor_copy(dst, window.indirect(offsets))
+            else:
+                nc.scalar.activation(dst, window.indirect(offsets), ACT.Copy)
+
+        def interleave_views(grouped, raw):
+            return (
+                grouped.rearrange("p (c i) j -> p c j i", i=4),
+                raw.rearrange("p j (c i) -> p c j i", i=4),
+            )
+
+        offs_sb = keep.tile([P, S // 16], U16, name="offs_sb")
+        pr_sb = [keep.tile([P, S // 16], U16, name="pr_sb%d" % r) for r in range(2)]
+        xw = keep.tile([P, T], I32, name="xw", align_bytes=64)
+        xs = keep.tile([P, T], U8, name="xs", align_bytes=64)
+        w1_raw = [keep.tile([P, PACK, HALF], F32, name="w1_raw%d" % h) for h in range(2)]
+        w2_raw = keep.tile([P, PACK, N], F32, name="w2_raw")
+        fin0 = [keep.tile([P, 2 * S], F32, name="fin0_%d" % t) for t in range(PACK)]
+        unit_sb = keep.tile([P, PACK], F32, name="unit_sb")
+        ident = keep.tile([P, P], F32, name="ident")
+
+        nc.vector.memset(xs[:].bitcast(I32), 0)
+        nc.sync.dma_start(offs_sb[:], offs)
+        nc.sync.dma_start(xw[:], x_words[0].rearrange("p n t -> p (n t)").bitcast(I32))
+        for q in range(4):
+            nc.sync.dma_start(
+                xs[32 * q : 32 * q + 4, :].bitcast(I32), x_scales[0][4 * q : 4 * q + 4, :].bitcast(I32)
+            )
+        w1_rows = w1.rearrange("(p j) c -> p j c", j=PACK)
+        for h in range(2):
+            nc.sync.dma_start(w1_raw[h][:], w1_rows[:, :, h * HALF : (h + 1) * HALF])
+        nc.sync.dma_start(w2_raw[:], w2.rearrange("(p j) c -> p j c", j=PACK))
+        nc.sync.dma_start(pr_sb[0][:], pr1)
+        nc.sync.dma_start(pr_sb[1][:], pr2)
+        rdy_rows = rdy.rearrange("(p t) c -> p t c", t=PACK)
+        for t in range(PACK):
+            nc.sync.dma_start(fin0[t][:, S : 2 * S], rdy_rows[:, t, :])
+        nc.sync.dma_start(unit_sb[:], unit.rearrange("(p t) o -> p (t o)", t=PACK))
+        make_identity(nc, ident[:])
+
+        xg_words = keep.tile([P, S], U32, name="xg_words", align_bytes=64)
+        xg_scales = keep.tile([P, S], U8, name="xg_scales", align_bytes=64)
+        nc.vector.tensor_copy(xg_words[:], xw[:].bitcast(U32).indirect(offs_sb[:]))
+        nc.vector.tensor_copy(xg_scales[:], xs[:].indirect(offs_sb[:]))
+
+        grown = keep.tile([P, PACK, PACK, 2, HALF // PACK], F32, name="grown")
+        excess = keep.tile([P, PACK, PACK, 2, HALF // PACK], F32, name="excess")
+        y_banks = {}
+        for h in range(2):
+            w1_bf = keep.tile([P, HALF, PACK], BF16, name="w1_bf%d" % h, align_bytes=64)
+            dst, src = interleave_views(w1_bf[:], w1_raw[h][:])
+            if h == 0:
+                nc.scalar.copy(dst, src)
+            else:
+                nc.vector.tensor_copy(dst, src)
+            w1_codes = keep.tile([P, HALF], U32, name="w1_codes%d" % h, align_bytes=64)
+            w1_scales = keep.tile([P, HALF], U8, name="w1_scales%d" % h, align_bytes=64)
+            nc.vector.quantize_mx(
+                out=w1_codes[:].bitcast(FP8X4), scales=w1_scales[:], in_=w1_bf[:].rearrange("p c j -> p (c j)")
+            )
+            for jp in range(2):
+                y_bank = psum.tile([P, 2, HALF], F32, name="y_bank", tag="bank%d" % (2 * h + jp))
+                y_banks[h, jp] = y_bank
+                for b in range(2):
+                    cols = slice((2 * jp + b) * P, (2 * jp + b + 1) * P)
+                    nc.tensor.matmul_mx(
+                        out=y_bank[:, b, :],
+                        lhsT=xg_words[:, cols].bitcast(FP8X4),
+                        lhsT_scale=xg_scales[:, cols],
+                        rhs=w1_codes[:].bitcast(FP8X4),
+                        rhs_scale=w1_scales[:],
+                        start=True,
+                        stop=True,
+                    )
+        for h in range(2):
+            for jp in range(2):
+                y_view = y_banks[h, jp][:].rearrange("p b (m t) -> p b t m", t=PACK)
+                nc.scalar.activation(
+                    grown[:, :, 2 * jp : 2 * jp + 2, h, :].rearrange("p t b m -> p b t m"), y_view, ACT.Exp
+                )
+                nc.vector.tensor_scalar(
+                    excess[:, :, 2 * jp : 2 * jp + 2, h, :].rearrange("p t b m -> p b t m"),
+                    y_view, KNEE, 0.0, ALU.subtract, ALU.max,
+                )
+
+        dur = [psum.tile([P, S], F32, name="dur%d" % t, tag="bank%d" % (4 + t)) for t in range(PACK)]
+        capped = []
+        for t in range(PACK):
+            cap_t = keep.tile([P, S], F32, name="capped%d" % t)
+            capped.append(cap_t)
+            nc.vector.tensor_scalar(
+                cap_t[:], grown[:, t].rearrange("p b h m -> p (b h m)"), math.e ** KNEE, None, ALU.min
+            )
+            for b in range(PACK):
+                nc.tensor.matmul(
+                    dur[t][:, b * P : (b + 1) * P],
+                    excess[:, t, b].rearrange("p h m -> p (h m)"),
+                    ident[:],
+                    start=(b == 0), stop=False, is_transpose=True,
+                )
+
+        w2_bf = keep.tile([P, N, PACK], BF16, name="w2_bf", align_bytes=64)
+        dst, src = interleave_views(w2_bf[:], w2_raw[:])
+        nc.vector.tensor_copy(dst, src)
+        w2_codes = keep.tile([P, N], U32, name="w2_codes", align_bytes=64)
+        w2_scales = keep.tile([P, N], U8, name="w2_scales", align_bytes=64)
+        nc.vector.quantize_mx(
+            out=w2_codes[:].bitcast(FP8X4), scales=w2_scales[:], in_=w2_bf[:].rearrange("p c j -> p (c j)")
+        )
+
+        for t in range(PACK):
+            soft = keep.tile([P, S], F32, name="soft%d" % t)
+            nc.scalar.activation(soft[:], capped[t][:], ACT.Ln, bias=1.0)
+            for b in range(PACK):
+                nc.tensor.matmul(
+                    dur[t][:, b * P : (b + 1) * P],
+                    soft[:, b * P : (b + 1) * P],
+                    ident[:],
+                    start=False, stop=(b == PACK - 1), is_transpose=True,
+                )
+            nc.vector.tensor_tensor(fin0[t][:, 0:S], fin0[t][:, S : 2 * S], dur[t][:], ALU.add)
+
+        fin1 = [keep.tile([P, 2 * S], F32, name="fin1_%d" % t) for t in range(PACK)]
+
+        def finish_round1(t):
+            nc.vector.tensor_tensor(fin1[t][:, 0:S], fin1[t][:, S : 2 * S], dur[t][:], ALU.add)
+
+        for t in range(PACK):
+            pair = [keep.tile([P, S], F32, name="first%d_%d" % (t, r)) for r in range(2)]
+            for r in range(2):
+                gather((t, r) in R1_ON_VECTOR, pair[r][:], fin0[t][:], pr_sb[r][:])
+            if t > 0:
+                finish_round1(t - 1)
+            nc.vector.tensor_tensor(fin1[t][:, S : 2 * S], pair[0][:], pair[1][:], ALU.max)
+
+        fin2 = keep.tile([P, PACK, S], F32, name="fin2")
+        later = [keep.tile([P, S], F32, name="later%d" % t) for t in range(PACK)]
+
+        def fetch_round2(t, cols, on_vector):
+            width = cols.stop - cols.start
+            lst = slice(cols.start // 16, cols.stop // 16)
+            pair = [keep.tile([P, width], F32, name="second%d_%d_%d" % (t, cols.start, r)) for r in range(2)]
+            for r in range(2):
+                gather((t, r) in on_vector, pair[r][:], fin1[t][:], pr_sb[r][:, lst])
+            nc.vector.tensor_tensor(later[t][:, cols], pair[0][:], pair[1][:], ALU.max)
+
+        def finish_round2(t, cols):
+            nc.vector.tensor_tensor(fin2[:, t, cols], later[t][:, cols], dur[t][:, cols], ALU.add)
+
+        def last_product(ci, cols, hid):
+            width = cols.stop - cols.start
+            hid_codes = keep.tile([P, width], U32, name="hid_codes%d" % ci, align_bytes=64)
+            hid_scales = keep.tile([P, width], U8, name="hid_scales%d" % ci, align_bytes=64)
+            nc.vector.quantize_mx(
+                out=hid_codes[:].bitcast(FP8X4), scales=hid_scales[:], in_=hid[:].rearrange("p c j -> p (c j)")
+            )
+            acc = psum.tile([P, 2, width], F32, name="acc", tag="bank%d" % ci)
+            for mh in range(2):
+                nc.tensor.matmul_mx(
+                    out=acc[:, mh, :],
+                    lhsT=w2_codes[:, mh * P : (mh + 1) * P].bitcast(FP8X4),
+                    lhsT_scale=w2_scales[:, mh * P : (mh + 1) * P],
+                    rhs=hid_codes[:].bitcast(FP8X4),
+                    rhs_scale=hid_scales[:],
+                    start=True,
+                    stop=True,
+                )
+            res = keep.tile([P, 2, width], F32, name="res%d" % ci)
+            nc.scalar.copy(res[:], acc[:])
+            nc.sync.dma_start(out.rearrange("(g p) c -> p g c", p=P)[:, :, cols], res[:])
+
+        every = slice(0, S)
+        for t in range(WHOLE):
+            fetch_round2(t, every, R2_ON_VECTOR)
+            if t == 0:
+                finish_round1(PACK - 1)
+            else:
+                finish_round2(t - 1, every)
+        c0 = 0
+        waiting = None
+        for ci, width in enumerate(CHUNKS):
+            cols = slice(c0, c0 + width)
+            for t in range(WHOLE, PACK):
+                fetch_round2(t, cols, ())
+            if waiting is None:
+                finish_round2(WHOLE - 1, every)
+            else:
+                last_product(*waiting)
+            for t in range(WHOLE, PACK):
+                finish_round2(t, cols)
+            hid = keep.tile([P, width, PACK], BF16, name="hid%d" % ci, align_bytes=64)
+            dst, src = interleave_views(hid[:], fin2[:, :, cols])
+            nc.vector.tensor_tensor(
+                dst, src, unit_sb[:].unsqueeze(1).unsqueeze(3).to_broadcast([P, width // 4, PACK, 4]), ALU.mult
+            )
+            waiting = (ci, cols, hid)
+            c0 = c0 + width
+        last_product(*waiting)

@@ -57,35 +57,33 @@ def tile_picked_ycritp_fin_p_kernel(
         unit_sb = keep.tile([P, PACK], F32, name="unit_sb")
         ident = keep.tile([P, P], F32, name="ident")
 
-        nc.vector.memset(xs[:].bitcast(I32), 0)
+        w1_rows = w1.rearrange("(p j) c -> p j c", j=PACK)
+        nc.gpsimd.memset(xs[:].bitcast(I32), 0)
+        nc.scalar.dma_start(w1_raw[0][:], w1_rows[:, :, 0:HALF])
         nc.sync.dma_start(offs_sb[:], offs)
-        nc.sync.dma_start(xw[:], x_words[0].rearrange("p n t -> p (n t)").bitcast(I32))
         for q in range(4):
             nc.sync.dma_start(
                 xs[32 * q : 32 * q + 4, :].bitcast(I32), x_scales[0][4 * q : 4 * q + 4, :].bitcast(I32)
             )
-        w1_rows = w1.rearrange("(p j) c -> p j c", j=PACK)
-        for h in range(2):
-            nc.sync.dma_start(w1_raw[h][:], w1_rows[:, :, h * HALF : (h + 1) * HALF])
-        nc.sync.dma_start(w2_raw[:], w2.rearrange("(p j) c -> p j c", j=PACK))
+        nc.sync.dma_start(xw[:], x_words[0].rearrange("p n t -> p (n t)").bitcast(I32))
+        nc.sync.dma_start(w1_raw[1][:], w1_rows[:, :, HALF:H])
         nc.sync.dma_start(pr_sb[0][:], pr1)
         nc.sync.dma_start(pr_sb[1][:], pr2)
         rdy_rows = rdy.rearrange("(p t) c -> p t c", t=PACK)
         for t in range(PACK):
             nc.sync.dma_start(fin0[t][:, S : 2 * S], rdy_rows[:, t, :])
+        nc.sync.dma_start(w2_raw[:], w2.rearrange("(p j) c -> p j c", j=PACK))
         nc.sync.dma_start(unit_sb[:], unit.rearrange("(p t) o -> p (t o)", t=PACK))
         make_identity(nc, ident[:])
 
-        xg_words = keep.tile([P, S], U32, name="xg_words", align_bytes=64)
+        xg_words = [keep.tile([P, S // 2], U32, name="xg_words%d" % jp, align_bytes=64) for jp in range(2)]
         xg_scales = keep.tile([P, S], U8, name="xg_scales", align_bytes=64)
-        nc.vector.tensor_copy(xg_words[:], xw[:].bitcast(U32).indirect(offs_sb[:]))
         nc.vector.tensor_copy(xg_scales[:], xs[:].indirect(offs_sb[:]))
 
         grown = keep.tile([P, PACK, PACK, 2, HALF // PACK], F32, name="grown")
-        excess = keep.tile([P, PACK, PACK, 2, HALF // PACK], F32, name="excess")
         y_banks = {}
         for h in range(2):
-            w1_bf = keep.tile([P, HALF, PACK], BF16, name="w1_bf%d" % h, align_bytes=64)
+            w1_bf = keep.tile([P, HALF, PACK], BF16, name="w1_bf%d" % h, tag="w1_bf%d" % h, align_bytes=64)
             dst, src = interleave_views(w1_bf[:], w1_raw[h][:])
             if h == 0:
                 nc.scalar.copy(dst, src)
@@ -97,19 +95,24 @@ def tile_picked_ycritp_fin_p_kernel(
                 out=w1_codes[:].bitcast(FP8X4), scales=w1_scales[:], in_=w1_bf[:].rearrange("p c j -> p (c j)")
             )
             for jp in range(2):
+                if h == 0:
+                    nc.vector.tensor_copy(
+                        xg_words[jp][:], xw[:].bitcast(U32).indirect(offs_sb[:, jp * 16 : (jp + 1) * 16])
+                    )
                 y_bank = psum.tile([P, 2, HALF], F32, name="y_bank", tag="bank%d" % (2 * h + jp))
                 y_banks[h, jp] = y_bank
                 for b in range(2):
                     cols = slice((2 * jp + b) * P, (2 * jp + b + 1) * P)
                     nc.tensor.matmul_mx(
                         out=y_bank[:, b, :],
-                        lhsT=xg_words[:, cols].bitcast(FP8X4),
+                        lhsT=xg_words[jp][:, b * P : (b + 1) * P].bitcast(FP8X4),
                         lhsT_scale=xg_scales[:, cols],
                         rhs=w1_codes[:].bitcast(FP8X4),
                         rhs_scale=w1_scales[:],
                         start=True,
                         stop=True,
                     )
+        excess = keep.tile([P, PACK, PACK, 2, HALF // PACK], F32, name="excess", tag="w1_bf1", align_bytes=64)
         for h in range(2):
             for jp in range(2):
                 y_view = y_banks[h, jp][:].rearrange("p b (m t) -> p b t m", t=PACK)
@@ -126,8 +129,8 @@ def tile_picked_ycritp_fin_p_kernel(
         for t in range(PACK):
             cap_t = keep.tile([P, S], F32, name="capped%d" % t)
             capped.append(cap_t)
-            nc.vector.tensor_scalar(
-                cap_t[:], grown[:, t].rearrange("p b h m -> p (b h m)"), math.e ** KNEE, None, ALU.min
+            nc.gpsimd.tensor_scalar(
+                cap_t[:], grown[:, t].rearrange("p b h m -> p (b h m)"), math.e ** KNEE, 0.0, ALU.min, ALU.max
             )
             for b in range(PACK):
                 nc.tensor.matmul(

from contextlib import ExitStack
import math

import concourse.mybir as mybir
from concourse.masks import make_identity

K, T, S, N, H = 512, 1024, 512, 256, 512
FLOPS = 2 * K * H * S + 2 * H * N * S

F32 = mybir.dt.float32
BF16 = mybir.dt.bfloat16
I32 = mybir.dt.int32
U32 = mybir.dt.uint32
U16 = mybir.dt.uint16
U8 = mybir.dt.uint8
FP8X4 = mybir.dt.float8_e4m3fn_x4
ALU = mybir.AluOpType
ACT = mybir.ActivationFunctionType

P = 128
PACK = 4
KNEE = 32.0
HALF = H // 2
CHUNKS = (128, 256, 128,)
R1_ON_VECTOR = {(0, 1), (1, 1), (2, 1)}
R2_ON_VECTOR = {(1, 1)}
WHOLE = 3


def tile_picked_ycritp_fin_p_kernel(
    tc, x_words, x_scales, w1, rdy, unit, w2, offs, pr1, pr2, out
):
    nc = tc.nc
    with ExitStack() as ctx:
        keep = ctx.enter_context(tc.tile_pool(name="keep", bufs=1))
        psum = ctx.enter_context(tc.psum_pool(name="psum", bufs=1))

        def gather(on_vector, dst, window, offsets):
            if on_vector:
                nc.vector.tensor_copy(dst, window.indirect(offsets))
            else:
                nc.scalar.activation(dst, window.indirect(offsets), ACT.Copy)

        def interleave_views(grouped, raw):
            return (
                grouped.rearrange("p (c i) j -> p c j i", i=4),
                raw.rearrange("p j (c i) -> p c j i", i=4),
            )

        offs_sb = keep.tile([P, S // 16], U16, name="offs_sb")
        pr_sb = [keep.tile([P, S // 16], U16, name="pr_sb%d" % r) for r in range(2)]
        xw = keep.tile([P, T], I32, name="xw", align_bytes=64)
        xs = keep.tile([P, T], U8, name="xs", align_bytes=64)
        w1_raw = [keep.tile([P, PACK, HALF], F32, name="w1_raw%d" % h) for h in range(2)]
        w2_raw = keep.tile([P, PACK, N], F32, name="w2_raw")
        fin0 = [keep.tile([P, 2 * S], F32, name="fin0_%d" % t) for t in range(PACK)]
        unit_sb = keep.tile([P, PACK], F32, name="unit_sb")
        ident = keep.tile([P, P], F32, name="ident")

        w1_rows = w1.rearrange("(p j) c -> p j c", j=PACK)
        nc.gpsimd.memset(xs[:].bitcast(I32), 0)
        nc.scalar.dma_start(w1_raw[0][:], w1_rows[:, :, 0:HALF])
        nc.sync.dma_start(offs_sb[:], offs)
        for q in range(4):
            nc.sync.dma_start(
                xs[32 * q : 32 * q + 4, :].bitcast(I32), x_scales[0][4 * q : 4 * q + 4, :].bitcast(I32)
            )
        nc.sync.dma_start(xw[:], x_words[0].rearrange("p n t -> p (n t)").bitcast(I32))
        nc.sync.dma_start(w1_raw[1][:], w1_rows[:, :, HALF:H])
        nc.sync.dma_start(pr_sb[0][:], pr1)
        nc.sync.dma_start(pr_sb[1][:], pr2)
        rdy_rows = rdy.rearrange("(p t) c -> p t c", t=PACK)
        for t in range(PACK):
            nc.sync.dma_start(fin0[t][:, S : 2 * S], rdy_rows[:, t, :])
        nc.sync.dma_start(w2_raw[:], w2.rearrange("(p j) c -> p j c", j=PACK))
        nc.sync.dma_start(unit_sb[:], unit.rearrange("(p t) o -> p (t o)", t=PACK))
        make_identity(nc, ident[:])

        xg_words = [keep.tile([P, S // 2], U32, name="xg_words%d" % jp, align_bytes=64) for jp in range(2)]
        xg_scales = keep.tile([P, S], U8, name="xg_scales", align_bytes=64)
        nc.vector.tensor_copy(xg_scales[:], xs[:].indirect(offs_sb[:]))

        grown = keep.tile([P, PACK, PACK, 2, HALF // PACK], F32, name="grown")
        y_banks = {}
        for h in range(2):
            w1_bf = keep.tile([P, HALF, PACK], BF16, name="w1_bf%d" % h, tag="w1_bf%d" % h, align_bytes=64)
            dst, src = interleave_views(w1_bf[:], w1_raw[h][:])
            if h == 0:
                nc.scalar.copy(dst, src)
            else:
                nc.vector.tensor_copy(dst, src)
            w1_codes = keep.tile([P, HALF], U32, name="w1_codes%d" % h, align_bytes=64)
            w1_scales = keep.tile([P, HALF], U8, name="w1_scales%d" % h, align_bytes=64)
            nc.vector.quantize_mx(
                out=w1_codes[:].bitcast(FP8X4), scales=w1_scales[:], in_=w1_bf[:].rearrange("p c j -> p (c j)")
            )
            for jp in range(2):
                if h == 0:
                    nc.vector.tensor_copy(
                        xg_words[jp][:], xw[:].bitcast(U32).indirect(offs_sb[:, jp * 16 : (jp + 1) * 16])
                    )
                y_bank = psum.tile([P, 2, HALF], F32, name="y_bank", tag="bank%d" % (2 * h + jp))
                y_banks[h, jp] = y_bank
                for b in range(2):
                    cols = slice((2 * jp + b) * P, (2 * jp + b + 1) * P)
                    nc.tensor.matmul_mx(
                        out=y_bank[:, b, :],
                        lhsT=xg_words[jp][:, b * P : (b + 1) * P].bitcast(FP8X4),
                        lhsT_scale=xg_scales[:, cols],
                        rhs=w1_codes[:].bitcast(FP8X4),
                        rhs_scale=w1_scales[:],
                        start=True,
                        stop=True,
                    )
        excess = keep.tile([P, PACK, PACK, 2, HALF // PACK], F32, name="excess", tag="w1_bf1", align_bytes=64)
        for h in range(2):
            for jp in range(2):
                y_view = y_banks[h, jp][:].rearrange("p b (m t) -> p b t m", t=PACK)
                nc.scalar.activation(
                    grown[:, :, 2 * jp : 2 * jp + 2, h, :].rearrange("p t b m -> p b t m"), y_view, ACT.Exp
                )
                nc.vector.tensor_scalar(
                    excess[:, :, 2 * jp : 2 * jp + 2, h, :].rearrange("p t b m -> p b t m"),
                    y_view, KNEE, 0.0, ALU.subtract, ALU.max,
                )

        dur = [psum.tile([P, S], F32, name="dur%d" % t, tag="bank%d" % (4 + t)) for t in range(PACK)]
        capped = []
        for t in range(PACK):
            cap_t = keep.tile([P, S], F32, name="capped%d" % t)
            capped.append(cap_t)
            nc.gpsimd.tensor_scalar(
                cap_t[:], grown[:, t].rearrange("p b h m -> p (b h m)"), math.e ** KNEE, 0.0, ALU.min, ALU.max
            )
            for b in range(PACK):
                nc.tensor.matmul(
                    dur[t][:, b * P : (b + 1) * P],
                    excess[:, t, b].rearrange("p h m -> p (h m)"),
                    ident[:],
                    start=(b == 0), stop=False, is_transpose=True,
                )

        w2_bf = keep.tile([P, N, PACK], BF16, name="w2_bf", align_bytes=64)
        dst, src = interleave_views(w2_bf[:], w2_raw[:])
        nc.vector.tensor_copy(dst, src)
        w2_codes = keep.tile([P, N], U32, name="w2_codes", align_bytes=64)
        w2_scales = keep.tile([P, N], U8, name="w2_scales", align_bytes=64)
        nc.vector.quantize_mx(
            out=w2_codes[:].bitcast(FP8X4), scales=w2_scales[:], in_=w2_bf[:].rearrange("p c j -> p (c j)")
        )

        for t in range(PACK):
            soft = keep.tile([P, S], F32, name="soft%d" % t)
            nc.scalar.activation(soft[:], capped[t][:], ACT.Ln, bias=1.0)
            for b in range(PACK):
                nc.tensor.matmul(
                    dur[t][:, b * P : (b + 1) * P],
                    soft[:, b * P : (b + 1) * P],
                    ident[:],
                    start=False, stop=(b == PACK - 1), is_transpose=True,
                )
            nc.vector.tensor_tensor(fin0[t][:, 0:S], fin0[t][:, S : 2 * S], dur[t][:], ALU.add)

        fin1 = [keep.tile([P, 2 * S], F32, name="fin1_%d" % t) for t in range(PACK)]

        def finish_round1(t):
            nc.vector.tensor_tensor(fin1[t][:, 0:S], fin1[t][:, S : 2 * S], dur[t][:], ALU.add)

        for t in range(PACK):
            pair = [keep.tile([P, S], F32, name="first%d_%d" % (t, r)) for r in range(2)]
            for r in range(2):
                gather((t, r) in R1_ON_VECTOR, pair[r][:], fin0[t][:], pr_sb[r][:])
            if t > 0:
                finish_round1(t - 1)
            nc.vector.tensor_tensor(fin1[t][:, S : 2 * S], pair[0][:], pair[1][:], ALU.max)

        fin2 = keep.tile([P, PACK, S], F32, name="fin2")
        later = [keep.tile([P, S], F32, name="later%d" % t) for t in range(PACK)]

        def fetch_round2(t, cols, on_vector):
            width = cols.stop - cols.start
            lst = slice(cols.start // 16, cols.stop // 16)
            pair = [keep.tile([P, width], F32, name="second%d_%d_%d" % (t, cols.start, r)) for r in range(2)]
            for r in range(2):
                gather((t, r) in on_vector, pair[r][:], fin1[t][:], pr_sb[r][:, lst])
            nc.vector.tensor_tensor(later[t][:, cols], pair[0][:], pair[1][:], ALU.max)

        def finish_round2(t, cols):
            nc.vector.tensor_tensor(fin2[:, t, cols], later[t][:, cols], dur[t][:, cols], ALU.add)

        def last_product(ci, cols, hid):
            width = cols.stop - cols.start
            hid_codes = keep.tile([P, width], U32, name="hid_codes%d" % ci, align_bytes=64)
            hid_scales = keep.tile([P, width], U8, name="hid_scales%d" % ci, align_bytes=64)
            nc.vector.quantize_mx(
                out=hid_codes[:].bitcast(FP8X4), scales=hid_scales[:], in_=hid[:].rearrange("p c j -> p (c j)")
            )
            acc = psum.tile([P, 2, width], F32, name="acc", tag="bank%d" % ci)
            for mh in range(2):
                nc.tensor.matmul_mx(
                    out=acc[:, mh, :],
                    lhsT=w2_codes[:, mh * P : (mh + 1) * P].bitcast(FP8X4),
                    lhsT_scale=w2_scales[:, mh * P : (mh + 1) * P],
                    rhs=hid_codes[:].bitcast(FP8X4),
                    rhs_scale=hid_scales[:],
                    start=True,
                    stop=True,
                )
            res = keep.tile([P, 2, width], F32, name="res%d" % ci)
            nc.scalar.copy(res[:], acc[:])
            nc.sync.dma_start(out.rearrange("(g p) c -> p g c", p=P)[:, :, cols], res[:])

        every = slice(0, S)
        for t in range(WHOLE):
            fetch_round2(t, every, R2_ON_VECTOR)
            if t == 0:
                finish_round1(PACK - 1)
            else:
                finish_round2(t - 1, every)
        c0 = 0
        waiting = None
        for ci, width in enumerate(CHUNKS):
            cols = slice(c0, c0 + width)
            for t in range(WHOLE, PACK):
                fetch_round2(t, cols, ())
            if waiting is None:
                finish_round2(WHOLE - 1, every)
            else:
                last_product(*waiting)
            for t in range(WHOLE, PACK):
                finish_round2(t, cols)
            hid = keep.tile([P, width, PACK], BF16, name="hid%d" % ci, align_bytes=64)
            dst, src = interleave_views(hid[:], fin2[:, :, cols])
            nc.vector.tensor_tensor(
                dst, src, unit_sb[:].unsqueeze(1).unsqueeze(3).to_broadcast([P, width // 4, PACK, 4]), ALU.mult
            )
            waiting = (ci, cols, hid)
            c0 = c0 + width
        last_product(*waiting)
